import numpy as np
import ml_dtypes


def mxq(x, axis, fmt="e4m3"):
    dtype, down = {"e4m3": (ml_dtypes.float8_e4m3fn, 7), "e5m2": (ml_dtypes.float8_e5m2, 14)}[fmt]
    v = np.moveaxis(np.asarray(x, np.float32).astype(ml_dtypes.bfloat16).astype(np.float64), axis, -1)
    blocks = v.reshape(v.shape[:-1] + (-1, 32))
    amax = np.abs(blocks).max(-1, keepdims=True)
    byte = np.maximum(np.where(amax > 0, np.frexp(amax)[1] - 1 + 127, 0) - down, 1)
    scale = np.exp2(byte - 127.0)
    codes = (blocks / scale).astype(np.float32).astype(dtype).astype(np.float64)
    return np.moveaxis((codes * scale).reshape(v.shape), -1, axis)


WIDE = False


def mx_kscale(k):
    if not WIDE:
        return np.ones(k)
    levels = np.array([10, -10, 5, -5, 0])
    if k % 512:
        return np.exp2(np.random.permutation(np.resize(levels, k // 32))).repeat(32)
    a = np.empty((k // 512, 16))
    for p in range(k // 512):
        a[p, :8] = np.random.permutation(np.resize(levels, 8))
        for g in range(8):
            far = levels[np.abs(levels - a[p, g]) >= 10]
            a[p, g + 8] = far[np.random.randint(len(far))]
    return np.exp2(a.ravel()).repeat(32)


BF16 = ml_dtypes.bfloat16


def bf(x):
    return np.asarray(x, np.float32).astype(BF16)


def f64(x):
    return np.asarray(x).astype(np.float64)


E2M1 = np.array([0.0, 0.5, 1.0, 1.5, 2.0, 3.0, 4.0, 6.0, -0.0, -0.5, -1.0, -1.5, -2.0, -3.0, -4.0, -6.0])


def pack_weight(w, fmt):
    k, n = w.shape
    w = f64(bf(w)).reshape(k // 32, 32, n)
    amax = np.abs(w).max(1)
    if fmt == "e4m3":
        byte = np.frexp(amax)[1] - 1 + 127 - 7
    else:
        mant, ex = np.frexp(amax / 6.0)
        byte = np.where(mant > 0.5, ex, ex - 1) + 127
    byte = np.clip(np.where(amax > 0, byte, 1), 1, 254)
    scaled = (w * np.exp2(127.0 - byte)[:, None, :]).reshape(k, n).astype(np.float32)
    by_word = np.ascontiguousarray(scaled.reshape(k // 512, 128, 4, n).transpose(0, 1, 3, 2))
    if fmt == "e4m3":
        words = by_word.astype(ml_dtypes.float8_e4m3fn).view(np.uint8)
    else:
        c = by_word.astype(ml_dtypes.float4_e2m1fn).view(np.uint8) & 0xF
        words = c[..., 0::2] | (c[..., 1::2] << 4)
    return np.ascontiguousarray(words), np.ascontiguousarray(byte.astype(np.uint8).reshape(k // 512, 16, n))


def unpack_weight(words, scales, fmt):
    g, p, n, _ = words.shape
    if fmt == "e4m3":
        vals = np.ascontiguousarray(words).view(ml_dtypes.float8_e4m3fn).astype(np.float64)
    else:
        nib = np.empty((g, p, n, 4), np.uint8)
        nib[..., 0::2] = words & 0xF
        nib[..., 1::2] = words >> 4
        vals = E2M1[nib]
    vals = vals * np.repeat(np.exp2(scales.astype(np.float64) - 127.0), 8, axis=1)[..., None]
    return vals.transpose(0, 1, 3, 2).reshape(g * 512, n)
def pack4(w):
    words, scales = pack_weight(w, "e2m1")
    return words.reshape(words.shape[0], 128, -1), scales


def unpack4(words, scales):
    return unpack_weight(words.reshape(words.shape[0], 128, -1, 2), scales, "e2m1")


M, K, N = 512, 1536, 2048


def setup_inputs():
    s = mx_kscale(K)
    root = np.sqrt(K)
    coef = np.random.standard_normal((M, K)) * s
    base = np.random.standard_normal((K, N)) / root / s[:, None]
    corr = 0.6 * np.random.standard_normal((K, N)) / root / s[:, None]
    update = 0.5 * np.random.standard_normal((K, N)) / root / s[:, None]
    base_words, base_scales = pack4(base)
    corr_words, corr_scales = pack_weight(corr, "e4m3")
    return {"alpha0": bf(np.random.standard_normal((M, N))),
            "coef": bf(coef),
            "base_words": base_words, "base_scales": base_scales,
            "corr_words": corr_words, "corr_scales": corr_scales,
            "update": bf(update)}


def reference(alpha0, coef, base_words, base_scales, corr_words, corr_scales, update):
    c = mxq(f64(coef), 1, "e4m3")
    explained_base = c @ unpack4(base_words, base_scales)
    explained_corr = c @ unpack_weight(corr_words, corr_scales, "e4m3")
    explained_update = c @ mxq(f64(update), 0, "e4m3")
    explained = explained_base + explained_corr + explained_update
    left = f64(alpha0) - explained
    return left * left

@@ -1,0 +1,243 @@
+from contextlib import ExitStack
+
+import concourse.mybir as mybir
+from concourse.masks import make_identity
+
+M, K, N = 512, 1536, 2048
+FLOPS = 3 * 2 * M * K * N
+
+F32 = mybir.dt.float32
+BF16 = mybir.dt.bfloat16
+I32 = mybir.dt.int32
+U32 = mybir.dt.uint32
+U8 = mybir.dt.uint8
+FP8X4 = mybir.dt.float8_e4m3fn_x4
+FP4X4 = mybir.dt.float4_e2m1fn_x4
+ALU = mybir.AluOpType
+ACT = mybir.ActivationFunctionType
+
+P = 128
+PACK = 4
+K_PASS = P * PACK
+PASSES = K // K_PASS
+ROW_TILES = M // P
+CHUNK = 512
+CHUNKS = N // CHUNK
+LOAD_RANGES = [(0, 512), (512, 1024), (1024, 2048)]
+SCALE_RANGES = [(0, 512), (512, 2048)]
+CORR_PLANE_ROW = 4
+VECTOR_COLS = 288
+ALIGN = 256
+
+
+def tile_batch_pursuit_scores_s10_kernel(
+    tc, alpha0, coef, base_words, base_scales, corr_words, corr_scales, update, out
+):
+    nc = tc.nc
+    with ExitStack() as ctx:
+        keep = ctx.enter_context(tc.tile_pool(name="keep", bufs=1))
+        stage = ctx.enter_context(tc.tile_pool(name="stage", bufs=3))
+        psum = ctx.enter_context(tc.psum_pool(name="psum", bufs=1))
+        ctx.enter_context(tc.manual_schedule())
+
+        def kept(name, shape, dtype):
+            return keep.tile(shape, dtype, name=name, align_bytes=ALIGN)
+
+        def bank(index, shape):
+            return psum.tile(shape, F32, name="bank", tag="bank%d" % index)
+
+        ident = kept("ident", [P, P], F32)
+        make_identity(nc, ident[:])
+
+        base_planes, corr_planes = [], []
+        for s, (n0, n1) in enumerate(SCALE_RANGES):
+            base_planes.append(kept("base_plane%d" % s, [P, PASSES, n1 - n0], U8))
+            corr_planes.append(kept("corr_plane%d" % s, [P, PASSES, n1 - n0], U8))
+            nc.vector.memset(base_planes[s][:].bitcast(I32), 0)
+            nc.vector.memset(corr_planes[s][:].bitcast(I32), 0)
+
+        def load_scale_rows(plane, first_row, scales, s, r):
+            n0, n1 = SCALE_RANGES[s]
+            nc.sync.dma_start(
+                out=plane[first_row + r : P : 32, :, :].bitcast(I32),
+                in_=scales[:, r:16:4, n0:n1].rearrange("g q n -> q g n").bitcast(I32),
+            )
+
+        coef_rows = coef.rearrange("(j p) k -> p j k", p=P)
+        alpha_rows = alpha0.rearrange("(j p) n -> p j n", p=P)
+        out_rows = out.rearrange("(j p) n -> p j n", p=P)
+        base_rows = base_words.rearrange("g p b -> p g b")
+        corr_rows = corr_words.rearrange("g p n t -> p g (n t)")
+
+        coef_raw, base_codes, corr_codes, update_raw, alpha_sb = {}, {}, {}, {}, {}
+
+        def load_coef(g):
+            coef_raw[g] = kept("coef_raw%d" % g, [P, ROW_TILES, K_PASS], BF16)
+            nc.sync.dma_start(out=coef_raw[g][:], in_=coef_rows[:, :, g * K_PASS : (g + 1) * K_PASS])
+
+        def load_base(i):
+            n0, n1 = LOAD_RANGES[i]
+            base_codes[i] = kept("base_codes%d" % i, [P, PASSES, 2 * (n1 - n0)], U8)
+            nc.sync.dma_start(out=base_codes[i][:].bitcast(I32), in_=base_rows[:, :, 2 * n0 : 2 * n1].bitcast(I32))
+
+        def load_corr(i):
+            n0, n1 = LOAD_RANGES[i]
+            corr_codes[i] = kept("corr_codes%d" % i, [P, PASSES, n1 - n0], U32)
+            nc.sync.dma_start(out=corr_codes[i][:].bitcast(I32), in_=corr_rows[:, :, 4 * n0 : 4 * n1].bitcast(I32))
+
+        def load_update_and_alpha(i):
+            n0, n1 = LOAD_RANGES[i]
+            for g in range(PASSES):
+                update_raw[i, g] = kept("update_raw%d_%d" % (i, g), [P, PACK, n1 - n0], BF16)
+                rows = update[g * K_PASS : (g + 1) * K_PASS, n0:n1]
+                nc.sync.dma_start(out=update_raw[i, g][:], in_=rows.rearrange("(p t) n -> p t n", t=PACK))
+            alpha_sb[i] = kept("alpha%d" % i, [P, ROW_TILES, n1 - n0], BF16)
+            nc.sync.dma_start(out=alpha_sb[i][:], in_=alpha_rows[:, :, n0:n1])
+
+        load_coef(0)
+        load_coef(1)
+        for r in range(4):
+            load_scale_rows(base_planes[0], 0, base_scales, 0, r)
+        load_base(0)
+        load_coef(2)
+        for r in range(4):
+            load_scale_rows(corr_planes[0], CORR_PLANE_ROW, corr_scales, 0, r)
+        load_corr(0)
+        load_update_and_alpha(0)
+        for r in range(4):
+            load_scale_rows(base_planes[1], 0, base_scales, 1, r)
+            load_scale_rows(corr_planes[1], CORR_PLANE_ROW, corr_scales, 1, r)
+        for i in range(1, len(LOAD_RANGES)):
+            load_base(i)
+            load_corr(i)
+            load_update_and_alpha(i)
+
+        def locate(ranges, c):
+            n0 = c * CHUNK
+            i = max(x for x in range(len(ranges)) if ranges[x][0] <= n0)
+            return i, n0 - ranges[i][0]
+
+        coef_codes, coef_scales, update_codes, update_scales = {}, {}, {}, {}
+
+        def prepare_coef(g):
+            coef_codes[g] = kept("coef_codes%d" % g, [P, M], U32)
+            coef_scales[g] = kept("coef_scales%d" % g, [P, M], U8)
+            for half in range(2):
+                turned = bank(4 + (2 * g + half) % 4, [P, 2, 2, P])
+                for jj in range(2):
+                    words = coef_raw[g][:, 2 * half + jj, :].bitcast(F32)
+                    for u in range(2):
+                        nc.tensor.transpose(turned[:, jj, u, :], words[:, u : 2 * P : 2], ident[:])
+                grouped = stage.tile([P, 2 * K_PASS], BF16, name="coef_grouped", align_bytes=ALIGN)
+                nc.scalar.copy(
+                    out=grouped[:].bitcast(F32).rearrange("p (j m u) -> p j m u", j=2, u=2),
+                    in_=turned[:].rearrange("p j u m -> p j m u"),
+                )
+                cols = slice(half * 2 * P, (half + 1) * 2 * P)
+                nc.vector.quantize_mx(
+                    out=coef_codes[g][:, cols].bitcast(FP8X4), scales=coef_scales[g][:, cols], in_=grouped[:]
+                )
+
+        def prepare_update(c, g):
+            i, off = locate(LOAD_RANGES, c)
+            grouped = stage.tile([P, CHUNK, PACK], BF16, name="update_grouped", align_bytes=ALIGN)
+            for copy, a, b in ((nc.vector.tensor_copy, 0, VECTOR_COLS), (nc.scalar.copy, VECTOR_COLS, CHUNK)):
+                copy(
+                    out=grouped[:, a:b, :].rearrange("p (c i) t -> p c t i", i=4),
+                    in_=update_raw[i, g][:, :, off + a : off + b].rearrange("p t (c i) -> p c t i", i=4),
+                )
+            update_codes[c, g] = kept("update_codes%d_%d" % (c, g), [P, CHUNK], U32)
+            update_scales[c, g] = kept("update_scales%d_%d" % (c, g), [P, CHUNK], U8)
+            nc.vector.quantize_mx(
+                out=update_codes[c, g][:].bitcast(FP8X4),
+                scales=update_scales[c, g][:],
+                in_=grouped[:].rearrange("p n t -> p (n t)"),
+            )
+
+        def moving(kind, c, g):
+            i, off = locate(LOAD_RANGES, c)
+            s, soff = locate(SCALE_RANGES, c)
+            if kind == "base":
+                return (
+                    base_codes[i][:, g, 2 * off : 2 * (off + CHUNK)].bitcast(FP4X4),
+                    base_planes[s][:, g, soff : soff + CHUNK],
+                )
+            if kind == "corr":
+                return (
+                    corr_codes[i][:, g, off : off + CHUNK].bitcast(FP8X4),
+                    corr_planes[s][CORR_PLANE_ROW:P, g, soff : soff + CHUNK],
+                )
+            return update_codes[c, g][:].bitcast(FP8X4), update_scales[c, g][:]
+
+        sums, results = {}, {}
+
+        def multiply(c, j, kind, g, start, stop):
+            if start:
+                sums[c, j] = bank(4 * (c % 2) + j, [P, CHUNK])
+            codes, scales = moving(kind, c, g)
+            cols = slice(j * P, (j + 1) * P)
+            nc.tensor.matmul_mx(
+                out=sums[c, j][:],
+                lhsT=coef_codes[g][:, cols].bitcast(FP8X4),
+                lhsT_scale=coef_scales[g][:, cols],
+                rhs=codes,
+                rhs_scale=scales,
+                start=start,
+                stop=stop,
+            )
+
+        def finish(c, j, a, b):
+            i, off = locate(LOAD_RANGES, c)
+            piece = results[c][:, j, a:b]
+            nc.vector.tensor_tensor(
+                out=piece, in0=alpha_sb[i][:, j, off + a : off + b], in1=sums[c, j][:, a:b], op=ALU.subtract
+            )
+            nc.scalar.activation(out=piece, in_=piece, func=ACT.Square)
+
+        def store(c, rows, a, b):
+            nc.sync.dma_start(out=out_rows[:, rows, c * CHUNK + a : c * CHUNK + b], in_=results[c][:, rows, a:b])
+
+        for c in range(CHUNKS):
+            results[c] = kept("result%d" % c, [P, ROW_TILES, CHUNK], F32)
+
+        terms = [(kind, g) for kind in ("base", "corr", "update") for g in range(PASSES)]
+
+        def sweep(c, some_terms, first, last):
+            for kind, g in some_terms:
+                for j in range(ROW_TILES):
+                    multiply(c, j, kind, g, (kind, g) == first, (kind, g) == last)
+
+        def finish_chunk(c):
+            for j in range(ROW_TILES):
+                finish(c, j, 0, CHUNK)
+            store(c, slice(0, ROW_TILES), 0, CHUNK)
+
+        first, last = terms[0], terms[-1]
+        prepare_coef(0)
+        prepare_coef(1)
+        sweep(0, [("base", 0), ("base", 1)], first, last)
+        prepare_coef(2)
+        for g in range(PASSES):
+            prepare_update(0, g)
+        sweep(0, [("corr", 0), ("corr", 1), ("base", 2), ("corr", 2)] + terms[2 * PASSES :], first, last)
+        finish_chunk(0)
+
+        for g in range(PASSES):
+            prepare_update(1, g)
+        sweep(1, terms, first, last)
+        finish_chunk(1)
+
+        for g in range(PASSES):
+            prepare_update(2, g)
+            prepare_update(3, g)
+        sweep(2, terms, first, last)
+        finish_chunk(2)
+
+        c = CHUNKS - 1
+        for j in range(ROW_TILES):
+            for term in terms:
+                multiply(c, j, term[0], term[1], term == first, term == last)
+            pieces = [(0, CHUNK)] if j < ROW_TILES - 1 else [(0, CHUNK // 2), (CHUNK // 2, CHUNK)]
+            for a, b in pieces:
+                finish(c, j, a, b)
+                store(c, slice(j, j + 1), a, b)

@@ -23,7 +23,8 @@ PASSES = K // K_PASS
 ROW_TILES = M // P
 CHUNK = 512
 CHUNKS = N // CHUNK
-LOAD_RANGES = [(0, 512), (512, 1024), (1024, 2048)]
+WARMUP_PASSES = 10
+TAIL_PIECES = [(0, 256), (256, 384), (384, 512)]
 SCALE_RANGES = [(0, 512), (512, 2048)]
 CORR_PLANE_ROW = 4
 VECTOR_COLS = 288
@@ -46,15 +47,32 @@ def tile_batch_pursuit_scores_s10_kernel(
         def bank(index, shape):
             return psum.tile(shape, F32, name="bank", tag="bank%d" % index)
 
-        ident = kept("ident", [P, P], F32)
-        make_identity(nc, ident[:])
-
         base_planes, corr_planes = [], []
         for s, (n0, n1) in enumerate(SCALE_RANGES):
             base_planes.append(kept("base_plane%d" % s, [P, PASSES, n1 - n0], U8))
             corr_planes.append(kept("corr_plane%d" % s, [P, PASSES, n1 - n0], U8))
-            nc.vector.memset(base_planes[s][:].bitcast(I32), 0)
-            nc.vector.memset(corr_planes[s][:].bitcast(I32), 0)
+        nc.gpsimd.memset(base_planes[0][:].bitcast(I32), 0)
+        ident = kept("ident", [P, P], F32)
+        make_identity(nc, ident[:])
+
+        ones = kept("ones", [P, K_PASS], BF16)
+        ones_codes = kept("ones_codes", [P, P], U32)
+        ones_scales = kept("ones_scales", [P, P], U8)
+        nc.vector.memset(ones[:], 1.0)
+        nc.vector.quantize_mx(out=ones_codes[:].bitcast(FP8X4), scales=ones_scales[:], in_=ones[:])
+        warm = bank(0, [P, P])
+        for w in range(WARMUP_PASSES):
+            nc.tensor.matmul_mx(
+                out=warm[:],
+                lhsT=ones_codes[:].bitcast(FP8X4),
+                lhsT_scale=ones_scales[:],
+                rhs=ones_codes[:].bitcast(FP8X4),
+                rhs_scale=ones_scales[:],
+                start=True,
+                stop=True,
+            )
+        for plane in (corr_planes[0], base_planes[1], corr_planes[1]):
+            nc.vector.memset(plane[:].bitcast(I32), 0)
 
         def load_scale_rows(plane, first_row, scales, s, r):
             n0, n1 = SCALE_RANGES[s]
@@ -71,46 +89,66 @@ def tile_batch_pursuit_scores_s10_kernel(
 
         coef_raw, base_codes, corr_codes, update_raw, alpha_sb = {}, {}, {}, {}, {}
 
-        def load_coef(g):
-            coef_raw[g] = kept("coef_raw%d" % g, [P, ROW_TILES, K_PASS], BF16)
-            nc.sync.dma_start(out=coef_raw[g][:], in_=coef_rows[:, :, g * K_PASS : (g + 1) * K_PASS])
+        def load_coef(g, j0, j1):
+            tile = kept("coef_raw%d_%d" % (g, j0), [P, j1 - j0, K_PASS], BF16)
+            nc.sync.dma_start(out=tile[:], in_=coef_rows[:, j0:j1, g * K_PASS : (g + 1) * K_PASS])
+            for j in range(j0, j1):
+                coef_raw[g, j] = tile[:, j - j0, :]
 
-        def load_base(i):
-            n0, n1 = LOAD_RANGES[i]
-            base_codes[i] = kept("base_codes%d" % i, [P, PASSES, 2 * (n1 - n0)], U8)
-            nc.sync.dma_start(out=base_codes[i][:].bitcast(I32), in_=base_rows[:, :, 2 * n0 : 2 * n1].bitcast(I32))
+        def load_base(c0, c1, g0, g1):
+            tile = kept("base_codes%d_%d" % (c0, g0), [P, g1 - g0, 2 * CHUNK * (c1 - c0)], U8)
+            nc.sync.dma_start(
+                out=tile[:].bitcast(I32), in_=base_rows[:, g0:g1, 2 * CHUNK * c0 : 2 * CHUNK * c1].bitcast(I32)
+            )
+            for c in range(c0, c1):
+                for g in range(g0, g1):
+                    base_codes[c, g] = tile[:, g - g0, 2 * CHUNK * (c - c0) : 2 * CHUNK * (c - c0 + 1)]
 
-        def load_corr(i):
-            n0, n1 = LOAD_RANGES[i]
-            corr_codes[i] = kept("corr_codes%d" % i, [P, PASSES, n1 - n0], U32)
-            nc.sync.dma_start(out=corr_codes[i][:].bitcast(I32), in_=corr_rows[:, :, 4 * n0 : 4 * n1].bitcast(I32))
+        def load_corr(c, g0, g1):
+            tile = kept("corr_codes%d_%d" % (c, g0), [P, g1 - g0, CHUNK], U32)
+            nc.sync.dma_start(
+                out=tile[:].bitcast(I32), in_=corr_rows[:, g0:g1, 4 * CHUNK * c : 4 * CHUNK * (c + 1)].bitcast(I32)
+            )
+            for g in range(g0, g1):
+                corr_codes[c, g] = tile[:, g - g0, :]
 
-        def load_update_and_alpha(i):
-            n0, n1 = LOAD_RANGES[i]
+        def load_update(c):
             for g in range(PASSES):
-                update_raw[i, g] = kept("update_raw%d_%d" % (i, g), [P, PACK, n1 - n0], BF16)
-                rows = update[g * K_PASS : (g + 1) * K_PASS, n0:n1]
-                nc.sync.dma_start(out=update_raw[i, g][:], in_=rows.rearrange("(p t) n -> p t n", t=PACK))
-            alpha_sb[i] = kept("alpha%d" % i, [P, ROW_TILES, n1 - n0], BF16)
-            nc.sync.dma_start(out=alpha_sb[i][:], in_=alpha_rows[:, :, n0:n1])
+                update_raw[c, g] = kept("update_raw%d_%d" % (c, g), [P, PACK, CHUNK], BF16)
+                rows = update[g * K_PASS : (g + 1) * K_PASS, c * CHUNK : (c + 1) * CHUNK]
+                nc.sync.dma_start(out=update_raw[c, g][:], in_=rows.rearrange("(p t) n -> p t n", t=PACK))
 
-        load_coef(0)
-        load_coef(1)
+        def load_alpha(c0, c1):
+            tile = kept("alpha%d" % c0, [P, ROW_TILES, CHUNK * (c1 - c0)], BF16)
+            nc.sync.dma_start(out=tile[:], in_=alpha_rows[:, :, CHUNK * c0 : CHUNK * c1])
+            for c in range(c0, c1):
+                alpha_sb[c] = tile[:, :, CHUNK * (c - c0) : CHUNK * (c - c0 + 1)]
+
+        load_coef(0, 0, 2)
+        load_coef(0, 2, 4)
         for r in range(4):
             load_scale_rows(base_planes[0], 0, base_scales, 0, r)
-        load_base(0)
-        load_coef(2)
+        load_base(0, 1, 0, 1)
+        load_coef(1, 0, 4)
         for r in range(4):
             load_scale_rows(corr_planes[0], CORR_PLANE_ROW, corr_scales, 0, r)
-        load_corr(0)
-        load_update_and_alpha(0)
+        load_corr(0, 0, 1)
+        load_coef(2, 0, 4)
+        load_base(0, 1, 1, PASSES)
+        load_corr(0, 1, PASSES)
+        load_update(0)
         for r in range(4):
             load_scale_rows(base_planes[1], 0, base_scales, 1, r)
             load_scale_rows(corr_planes[1], CORR_PLANE_ROW, corr_scales, 1, r)
-        for i in range(1, len(LOAD_RANGES)):
-            load_base(i)
-            load_corr(i)
-            load_update_and_alpha(i)
+        load_base(1, 2, 0, PASSES)
+        load_corr(1, 0, PASSES)
+        load_update(1)
+        load_alpha(0, 2)
+        load_base(2, 4, 0, PASSES)
+        for c in (2, 3):
+            load_corr(c, 0, PASSES)
+            load_update(c)
+        load_alpha(2, 4)
 
         def locate(ranges, c):
             n0 = c * CHUNK
@@ -119,32 +157,31 @@ def tile_batch_pursuit_scores_s10_kernel(
 
         coef_codes, coef_scales, update_codes, update_scales = {}, {}, {}, {}
 
-        def prepare_coef(g):
+        def prepare_coef(g, tiles_per_bank, first_bank):
             coef_codes[g] = kept("coef_codes%d" % g, [P, M], U32)
             coef_scales[g] = kept("coef_scales%d" % g, [P, M], U8)
-            for half in range(2):
-                turned = bank(4 + (2 * g + half) % 4, [P, 2, 2, P])
-                for jj in range(2):
-                    words = coef_raw[g][:, 2 * half + jj, :].bitcast(F32)
+            for part in range(ROW_TILES // tiles_per_bank):
+                turned = bank(first_bank + part, [P, tiles_per_bank, 2, P])
+                for jj in range(tiles_per_bank):
+                    words = coef_raw[g, tiles_per_bank * part + jj].bitcast(F32)
                     for u in range(2):
                         nc.tensor.transpose(turned[:, jj, u, :], words[:, u : 2 * P : 2], ident[:])
-                grouped = stage.tile([P, 2 * K_PASS], BF16, name="coef_grouped", align_bytes=ALIGN)
+                grouped = stage.tile([P, tiles_per_bank * K_PASS], BF16, name="coef_grouped", align_bytes=ALIGN)
                 nc.scalar.copy(
-                    out=grouped[:].bitcast(F32).rearrange("p (j m u) -> p j m u", j=2, u=2),
+                    out=grouped[:].bitcast(F32).rearrange("p (j m u) -> p j m u", j=tiles_per_bank, u=2),
                     in_=turned[:].rearrange("p j u m -> p j m u"),
                 )
-                cols = slice(half * 2 * P, (half + 1) * 2 * P)
+                cols = slice(part * tiles_per_bank * P, (part + 1) * tiles_per_bank * P)
                 nc.vector.quantize_mx(
                     out=coef_codes[g][:, cols].bitcast(FP8X4), scales=coef_scales[g][:, cols], in_=grouped[:]
                 )
 
         def prepare_update(c, g):
-            i, off = locate(LOAD_RANGES, c)
             grouped = stage.tile([P, CHUNK, PACK], BF16, name="update_grouped", align_bytes=ALIGN)
             for copy, a, b in ((nc.vector.tensor_copy, 0, VECTOR_COLS), (nc.scalar.copy, VECTOR_COLS, CHUNK)):
                 copy(
                     out=grouped[:, a:b, :].rearrange("p (c i) t -> p c t i", i=4),
-                    in_=update_raw[i, g][:, :, off + a : off + b].rearrange("p t (c i) -> p c t i", i=4),
+                    in_=update_raw[c, g][:, :, a:b].rearrange("p t (c i) -> p c t i", i=4),
                 )
             update_codes[c, g] = kept("update_codes%d_%d" % (c, g), [P, CHUNK], U32)
             update_scales[c, g] = kept("update_scales%d_%d" % (c, g), [P, CHUNK], U8)
@@ -155,16 +192,15 @@ def tile_batch_pursuit_scores_s10_kernel(
             )
 
         def moving(kind, c, g):
-            i, off = locate(LOAD_RANGES, c)
             s, soff = locate(SCALE_RANGES, c)
             if kind == "base":
                 return (
-                    base_codes[i][:, g, 2 * off : 2 * (off + CHUNK)].bitcast(FP4X4),
+                    base_codes[c, g].bitcast(FP4X4),
                     base_planes[s][:, g, soff : soff + CHUNK],
                 )
             if kind == "corr":
                 return (
-                    corr_codes[i][:, g, off : off + CHUNK].bitcast(FP8X4),
+                    corr_codes[c, g].bitcast(FP8X4),
                     corr_planes[s][CORR_PLANE_ROW:P, g, soff : soff + CHUNK],
                 )
             return update_codes[c, g][:].bitcast(FP8X4), update_scales[c, g][:]
@@ -187,10 +223,9 @@ def tile_batch_pursuit_scores_s10_kernel(
             )
 
         def finish(c, j, a, b):
-            i, off = locate(LOAD_RANGES, c)
             piece = results[c][:, j, a:b]
             nc.vector.tensor_tensor(
-                out=piece, in0=alpha_sb[i][:, j, off + a : off + b], in1=sums[c, j][:, a:b], op=ALU.subtract
+                out=piece, in0=alpha_sb[c][:, j, a:b], in1=sums[c, j][:, a:b], op=ALU.subtract
             )
             nc.scalar.activation(out=piece, in_=piece, func=ACT.Square)
 
@@ -213,31 +248,52 @@ def tile_batch_pursuit_scores_s10_kernel(
             store(c, slice(0, ROW_TILES), 0, CHUNK)
 
         first, last = terms[0], terms[-1]
-        prepare_coef(0)
-        prepare_coef(1)
-        sweep(0, [("base", 0), ("base", 1)], first, last)
-        prepare_coef(2)
+        prepare_coef(0, 1, 4)
+        sweep(0, [("base", 0)], first, last)
+        prepare_coef(1, 2, 4)
+        sweep(0, [("corr", 0)], first, last)
+        prepare_coef(2, 2, 6)
         for g in range(PASSES):
             prepare_update(0, g)
-        sweep(0, [("corr", 0), ("corr", 1), ("base", 2), ("corr", 2)] + terms[2 * PASSES :], first, last)
-        finish_chunk(0)
+        sweep(0, [("base", 1), ("corr", 1), ("base", 2), ("corr", 2)] + terms[2 * PASSES :], first, last)
 
-        for g in range(PASSES):
-            prepare_update(1, g)
-        sweep(1, terms, first, last)
-        finish_chunk(1)
-
-        for g in range(PASSES):
-            prepare_update(2, g)
-            prepare_update(3, g)
-        sweep(2, terms, first, last)
-        finish_chunk(2)
+        for c in (1, 2):
+            for g in range(PASSES):
+                prepare_update(c, g)
+            finish_chunk(c - 1)
+            sweep(c, terms, first, last)
 
         c = CHUNKS - 1
-        for j in range(ROW_TILES):
-            for term in terms:
-                multiply(c, j, term[0], term[1], term == first, term == last)
-            pieces = [(0, CHUNK)] if j < ROW_TILES - 1 else [(0, CHUNK // 2), (CHUNK // 2, CHUNK)]
-            for a, b in pieces:
-                finish(c, j, a, b)
-                store(c, slice(j, j + 1), a, b)
+        for g in range(PASSES):
+            prepare_update(c, g)
+        finish_chunk(c - 1)
+        last_tile = ROW_TILES - 1
+        for term in terms[:PASSES]:
+            for j in range(ROW_TILES):
+                multiply(c, j, term[0], term[1], term == first, j == last_tile and term == terms[PASSES - 1])
+        tail = results[c][:, last_tile, :]
+        nc.vector.tensor_tensor(
+            out=tail, in0=alpha_sb[c][:, last_tile, :], in1=sums[c, last_tile][:], op=ALU.subtract
+        )
+        for j in range(last_tile):
+            for term in terms[PASSES:]:
+                multiply(c, j, term[0], term[1], False, term == last)
+            finish(c, j, 0, CHUNK)
+            store(c, slice(j, j + 1), 0, CHUNK)
+        cols = slice(last_tile * P, M)
+        for index, (a, b) in enumerate(TAIL_PIECES):
+            rest = bank(index, [P, b - a])
+            for kind, g in terms[PASSES:]:
+                codes, scales = moving(kind, c, g)
+                nc.tensor.matmul_mx(
+                    out=rest[:],
+                    lhsT=coef_codes[g][:, cols].bitcast(FP8X4),
+                    lhsT_scale=coef_scales[g][:, cols],
+                    rhs=codes[:, a:b],
+                    rhs_scale=scales[:, a:b],
+                    start=(kind, g) == terms[PASSES],
+                    stop=(kind, g) == last,
+                )
+            nc.vector.tensor_tensor(out=tail[:, a:b], in0=tail[:, a:b], in1=rest[:], op=ALU.subtract)
+            nc.scalar.activation(out=tail[:, a:b], in_=tail[:, a:b], func=ACT.Square)
+            store(c, slice(last_tile, ROW_TILES), a, b)

@@ -25,7 +25,7 @@ CHUNK = 512
 CHUNKS = N // CHUNK
 WARMUP_PASSES = 10
 TAIL_PIECES = [(0, 256), (256, 384), (384, 512)]
-SCALE_RANGES = [(0, 512), (512, 2048)]
+SCALE_RANGES = [(0, 512), (512, 1024), (1024, 2048)]
 CORR_PLANE_ROW = 4
 VECTOR_COLS = 288
 ALIGN = 256
@@ -71,7 +71,7 @@ def tile_batch_pursuit_scores_s10_kernel(
                 start=True,
                 stop=True,
             )
-        for plane in (corr_planes[0], base_planes[1], corr_planes[1]):
+        for plane in [corr_planes[0]] + base_planes[1:] + corr_planes[1:]:
             nc.vector.memset(plane[:].bitcast(I32), 0)
 
         def load_scale_rows(plane, first_row, scales, s, r):
@@ -112,11 +112,19 @@ def tile_batch_pursuit_scores_s10_kernel(
             for g in range(g0, g1):
                 corr_codes[c, g] = tile[:, g - g0, :]
 
-        def load_update(c):
-            for g in range(PASSES):
+        def load_update(c, g0=0, g1=PASSES):
+            for g in range(g0, g1):
                 update_raw[c, g] = kept("update_raw%d_%d" % (c, g), [P, PACK, CHUNK], BF16)
                 rows = update[g * K_PASS : (g + 1) * K_PASS, c * CHUNK : (c + 1) * CHUNK]
                 nc.sync.dma_start(out=update_raw[c, g][:], in_=rows.rearrange("(p t) n -> p t n", t=PACK))
+
+        def load_base_scales(s):
+            for r in range(4):
+                load_scale_rows(base_planes[s], 0, base_scales, s, r)
+
+        def load_corr_scales(s):
+            for r in range(4):
+                load_scale_rows(corr_planes[s], CORR_PLANE_ROW, corr_scales, s, r)
 
         def load_alpha(c0, c1):
             tile = kept("alpha%d" % c0, [P, ROW_TILES, CHUNK * (c1 - c0)], BF16)
@@ -126,28 +134,30 @@ def tile_batch_pursuit_scores_s10_kernel(
 
         load_coef(0, 0, 2)
         load_coef(0, 2, 4)
-        for r in range(4):
-            load_scale_rows(base_planes[0], 0, base_scales, 0, r)
+        load_base_scales(0)
         load_base(0, 1, 0, 1)
         load_coef(1, 0, 4)
-        for r in range(4):
-            load_scale_rows(corr_planes[0], CORR_PLANE_ROW, corr_scales, 0, r)
+        load_corr_scales(0)
         load_corr(0, 0, 1)
         load_coef(2, 0, 4)
         load_base(0, 1, 1, PASSES)
         load_corr(0, 1, PASSES)
-        load_update(0)
-        for r in range(4):
-            load_scale_rows(base_planes[1], 0, base_scales, 1, r)
-            load_scale_rows(corr_planes[1], CORR_PLANE_ROW, corr_scales, 1, r)
+        load_update(0, 0, 1)
+        load_base_scales(1)
+        load_update(0, 1, PASSES)
         load_base(1, 2, 0, PASSES)
+        load_corr_scales(1)
         load_corr(1, 0, PASSES)
         load_update(1)
-        load_alpha(0, 2)
+        load_base_scales(2)
+        load_alpha(0, 1)
         load_base(2, 4, 0, PASSES)
-        for c in (2, 3):
-            load_corr(c, 0, PASSES)
-            load_update(c)
+        load_corr_scales(2)
+        load_corr(2, 0, PASSES)
+        load_update(2)
+        load_alpha(1, 2)
+        load_corr(3, 0, PASSES)
+        load_update(3)
         load_alpha(2, 4)
 
         def locate(ranges, c):

@@ -13,8 +13,8 @@ U32 = mybir.dt.uint32
 U8 = mybir.dt.uint8
 FP8X4 = mybir.dt.float8_e4m3fn_x4
 FP4X4 = mybir.dt.float4_e2m1fn_x4
-ALU = mybir.AluOpType
-ACT = mybir.ActivationFunctionType
+SUBTRACT = mybir.AluOpType.subtract
+SQUARE = mybir.ActivationFunctionType.Square
 
 P = 128
 PACK = 4
@@ -22,13 +22,16 @@ K_PASS = P * PACK
 PASSES = K // K_PASS
 ROW_TILES = M // P
 CHUNK = 512
-CHUNKS = N // CHUNK
-WARMUP_PASSES = 10
-TAIL_PIECES = [(0, 256), (256, 384), (384, 512)]
-SCALE_RANGES = [(0, 512), (512, 1024), (1024, 2048)]
-CORR_PLANE_ROW = 4
-VECTOR_COLS = 288
+QUADRANT = 32
+SCALE_ROWS = 4
 ALIGN = 256
+
+SCALE_RANGES = [(0, 1), (1, 2), (2, 4)]
+CORR_PLANE_ROW = 4
+VECTOR_COLS = 256
+STAGE_BUFS = 3
+BANK_HALVES = [(0, 256), (256, 512)]
+LAST_GROUPS = [(0, 256), (256, 384), (384, 512)]
 
 
 def tile_batch_pursuit_scores_s10_kernel(
@@ -37,7 +40,7 @@ def tile_batch_pursuit_scores_s10_kernel(
     nc = tc.nc
     with ExitStack() as ctx:
         keep = ctx.enter_context(tc.tile_pool(name="keep", bufs=1))
-        stage = ctx.enter_context(tc.tile_pool(name="stage", bufs=3))
+        stage = ctx.enter_context(tc.tile_pool(name="stage", bufs=STAGE_BUFS))
         psum = ctx.enter_context(tc.psum_pool(name="psum", bufs=1))
         ctx.enter_context(tc.manual_schedule())
 
@@ -48,38 +51,14 @@ def tile_batch_pursuit_scores_s10_kernel(
             return psum.tile(shape, F32, name="bank", tag="bank%d" % index)
 
         base_planes, corr_planes = [], []
-        for s, (n0, n1) in enumerate(SCALE_RANGES):
-            base_planes.append(kept("base_plane%d" % s, [P, PASSES, n1 - n0], U8))
-            corr_planes.append(kept("corr_plane%d" % s, [P, PASSES, n1 - n0], U8))
+        for s, (c0, c1) in enumerate(SCALE_RANGES):
+            base_planes.append(kept("base_plane%d" % s, [P, PASSES, CHUNK * (c1 - c0)], U8))
+            corr_planes.append(kept("corr_plane%d" % s, [P, PASSES, CHUNK * (c1 - c0)], U8))
         nc.gpsimd.memset(base_planes[0][:].bitcast(I32), 0)
         ident = kept("ident", [P, P], F32)
         make_identity(nc, ident[:])
-
-        ones = kept("ones", [P, K_PASS], BF16)
-        ones_codes = kept("ones_codes", [P, P], U32)
-        ones_scales = kept("ones_scales", [P, P], U8)
-        nc.vector.memset(ones[:], 1.0)
-        nc.vector.quantize_mx(out=ones_codes[:].bitcast(FP8X4), scales=ones_scales[:], in_=ones[:])
-        warm = bank(0, [P, P])
-        for w in range(WARMUP_PASSES):
-            nc.tensor.matmul_mx(
-                out=warm[:],
-                lhsT=ones_codes[:].bitcast(FP8X4),
-                lhsT_scale=ones_scales[:],
-                rhs=ones_codes[:].bitcast(FP8X4),
-                rhs_scale=ones_scales[:],
-                start=True,
-                stop=True,
-            )
         for plane in [corr_planes[0]] + base_planes[1:] + corr_planes[1:]:
             nc.vector.memset(plane[:].bitcast(I32), 0)
-
-        def load_scale_rows(plane, first_row, scales, s, r):
-            n0, n1 = SCALE_RANGES[s]
-            nc.sync.dma_start(
-                out=plane[first_row + r : P : 32, :, :].bitcast(I32),
-                in_=scales[:, r:16:4, n0:n1].rearrange("g q n -> q g n").bitcast(I32),
-            )
 
         coef_rows = coef.rearrange("(j p) k -> p j k", p=P)
         alpha_rows = alpha0.rearrange("(j p) n -> p j n", p=P)
@@ -88,6 +67,21 @@ def tile_batch_pursuit_scores_s10_kernel(
         corr_rows = corr_words.rearrange("g p n t -> p g (n t)")
 
         coef_raw, base_codes, corr_codes, update_raw, alpha_sb = {}, {}, {}, {}, {}
+
+        def load_scales(plane, first_row, scales, s):
+            c0, c1 = SCALE_RANGES[s]
+            for r in range(SCALE_ROWS):
+                rows = scales[:, r : K_PASS // 32 : SCALE_ROWS, CHUNK * c0 : CHUNK * c1]
+                nc.sync.dma_start(
+                    out=plane[first_row + r : P : QUADRANT, :, :].bitcast(I32),
+                    in_=rows.rearrange("g q n -> q g n").bitcast(I32),
+                )
+
+        def load_base_scales(s):
+            load_scales(base_planes[s], 0, base_scales, s)
+
+        def load_corr_scales(s):
+            load_scales(corr_planes[s], CORR_PLANE_ROW, corr_scales, s)
 
         def load_coef(g, j0, j1):
             tile = kept("coef_raw%d_%d" % (g, j0), [P, j1 - j0, K_PASS], BF16)
@@ -104,27 +98,22 @@ def tile_batch_pursuit_scores_s10_kernel(
                 for g in range(g0, g1):
                     base_codes[c, g] = tile[:, g - g0, 2 * CHUNK * (c - c0) : 2 * CHUNK * (c - c0 + 1)]
 
-        def load_corr(c, g0, g1):
-            tile = kept("corr_codes%d_%d" % (c, g0), [P, g1 - g0, CHUNK], U32)
+        def load_corr(c0, c1, g0, g1):
+            tile = kept("corr_codes%d_%d" % (c0, g0), [P, g1 - g0, CHUNK * (c1 - c0)], U32)
             nc.sync.dma_start(
-                out=tile[:].bitcast(I32), in_=corr_rows[:, g0:g1, 4 * CHUNK * c : 4 * CHUNK * (c + 1)].bitcast(I32)
+                out=tile[:].bitcast(I32), in_=corr_rows[:, g0:g1, 4 * CHUNK * c0 : 4 * CHUNK * c1].bitcast(I32)
             )
-            for g in range(g0, g1):
-                corr_codes[c, g] = tile[:, g - g0, :]
+            for c in range(c0, c1):
+                for g in range(g0, g1):
+                    corr_codes[c, g] = tile[:, g - g0, CHUNK * (c - c0) : CHUNK * (c - c0 + 1)]
 
-        def load_update(c, g0=0, g1=PASSES):
-            for g in range(g0, g1):
-                update_raw[c, g] = kept("update_raw%d_%d" % (c, g), [P, PACK, CHUNK], BF16)
-                rows = update[g * K_PASS : (g + 1) * K_PASS, c * CHUNK : (c + 1) * CHUNK]
-                nc.sync.dma_start(out=update_raw[c, g][:], in_=rows.rearrange("(p t) n -> p t n", t=PACK))
-
-        def load_base_scales(s):
-            for r in range(4):
-                load_scale_rows(base_planes[s], 0, base_scales, s, r)
-
-        def load_corr_scales(s):
-            for r in range(4):
-                load_scale_rows(corr_planes[s], CORR_PLANE_ROW, corr_scales, s, r)
+        def load_update(c0, c1):
+            for g in range(PASSES):
+                tile = kept("update_raw%d_%d" % (c0, g), [P, PACK, CHUNK * (c1 - c0)], BF16)
+                rows = update[g * K_PASS : (g + 1) * K_PASS, CHUNK * c0 : CHUNK * c1]
+                nc.sync.dma_start(out=tile[:], in_=rows.rearrange("(p t) n -> p t n", t=PACK))
+                for c in range(c0, c1):
+                    update_raw[c, g] = tile[:, :, CHUNK * (c - c0) : CHUNK * (c - c0 + 1)]
 
         def load_alpha(c0, c1):
             tile = kept("alpha%d" % c0, [P, ROW_TILES, CHUNK * (c1 - c0)], BF16)
@@ -133,37 +122,27 @@ def tile_batch_pursuit_scores_s10_kernel(
                 alpha_sb[c] = tile[:, :, CHUNK * (c - c0) : CHUNK * (c - c0 + 1)]
 
         load_coef(0, 0, 2)
-        load_coef(0, 2, 4)
+        load_coef(0, 2, ROW_TILES)
         load_base_scales(0)
         load_base(0, 1, 0, 1)
-        load_coef(1, 0, 4)
+        load_coef(1, 0, ROW_TILES)
         load_corr_scales(0)
-        load_corr(0, 0, 1)
-        load_coef(2, 0, 4)
+        load_corr(0, 1, 0, 1)
+        load_coef(2, 0, ROW_TILES)
         load_base(0, 1, 1, PASSES)
-        load_corr(0, 1, PASSES)
-        load_update(0, 0, 1)
+        load_corr(0, 1, 1, PASSES)
         load_base_scales(1)
-        load_update(0, 1, PASSES)
         load_base(1, 2, 0, PASSES)
         load_corr_scales(1)
-        load_corr(1, 0, PASSES)
-        load_update(1)
+        load_corr(1, 2, 0, PASSES)
+        load_update(0, 2)
+        load_alpha(0, 2)
         load_base_scales(2)
-        load_alpha(0, 1)
         load_base(2, 4, 0, PASSES)
+        load_update(2, 4)
         load_corr_scales(2)
-        load_corr(2, 0, PASSES)
-        load_update(2)
-        load_alpha(1, 2)
-        load_corr(3, 0, PASSES)
-        load_update(3)
+        load_corr(2, 4, 0, PASSES)
         load_alpha(2, 4)
-
-        def locate(ranges, c):
-            n0 = c * CHUNK
-            i = max(x for x in range(len(ranges)) if ranges[x][0] <= n0)
-            return i, n0 - ranges[i][0]
 
         coef_codes, coef_scales, update_codes, update_scales = {}, {}, {}, {}
 
@@ -173,26 +152,29 @@ def tile_batch_pursuit_scores_s10_kernel(
             for part in range(ROW_TILES // tiles_per_bank):
                 turned = bank(first_bank + part, [P, tiles_per_bank, 2, P])
                 for jj in range(tiles_per_bank):
-                    words = coef_raw[g, tiles_per_bank * part + jj].bitcast(F32)
+                    pairs = coef_raw[g, tiles_per_bank * part + jj].bitcast(F32)
                     for u in range(2):
-                        nc.tensor.transpose(turned[:, jj, u, :], words[:, u : 2 * P : 2], ident[:])
+                        nc.tensor.transpose(turned[:, jj, u, :], pairs[:, u : 2 * P : 2], ident[:])
                 grouped = stage.tile([P, tiles_per_bank * K_PASS], BF16, name="coef_grouped", align_bytes=ALIGN)
                 nc.scalar.copy(
                     out=grouped[:].bitcast(F32).rearrange("p (j m u) -> p j m u", j=tiles_per_bank, u=2),
                     in_=turned[:].rearrange("p j u m -> p j m u"),
                 )
-                cols = slice(part * tiles_per_bank * P, (part + 1) * tiles_per_bank * P)
+                rows = slice(part * tiles_per_bank * P, (part + 1) * tiles_per_bank * P)
                 nc.vector.quantize_mx(
-                    out=coef_codes[g][:, cols].bitcast(FP8X4), scales=coef_scales[g][:, cols], in_=grouped[:]
+                    out=coef_codes[g][:, rows].bitcast(FP8X4), scales=coef_scales[g][:, rows], in_=grouped[:]
                 )
 
-        def prepare_update(c, g):
+        def interleave_update(c, g):
             grouped = stage.tile([P, CHUNK, PACK], BF16, name="update_grouped", align_bytes=ALIGN)
             for copy, a, b in ((nc.vector.tensor_copy, 0, VECTOR_COLS), (nc.scalar.copy, VECTOR_COLS, CHUNK)):
                 copy(
-                    out=grouped[:, a:b, :].rearrange("p (c i) t -> p c t i", i=4),
-                    in_=update_raw[c, g][:, :, a:b].rearrange("p t (c i) -> p c t i", i=4),
+                    out=grouped[:, a:b, :].rearrange("p (n i) t -> p n t i", i=4),
+                    in_=update_raw[c, g][:, :, a:b].rearrange("p t (n i) -> p n t i", i=4),
                 )
+            return grouped
+
+        def quantize_update(c, g, grouped):
             update_codes[c, g] = kept("update_codes%d_%d" % (c, g), [P, CHUNK], U32)
             update_scales[c, g] = kept("update_scales%d_%d" % (c, g), [P, CHUNK], U8)
             nc.vector.quantize_mx(
@@ -201,109 +183,119 @@ def tile_batch_pursuit_scores_s10_kernel(
                 in_=grouped[:].rearrange("p n t -> p (n t)"),
             )
 
-        def moving(kind, c, g):
-            s, soff = locate(SCALE_RANGES, c)
+        def prepare_update(chunks):
+            waiting = None
+            for g in range(PASSES):
+                for c in chunks:
+                    grouped = interleave_update(c, g)
+                    if waiting is not None:
+                        quantize_update(*waiting)
+                    waiting = (c, g, grouped)
+            quantize_update(*waiting)
+
+        base_terms = [("base", g) for g in range(PASSES)]
+        corr_terms = [("corr", g) for g in range(PASSES)]
+        update_terms = [("update", g) for g in range(PASSES)]
+
+        def moving_operand(term, c):
+            kind, g = term
+            if kind == "update":
+                return update_codes[c, g][:].bitcast(FP8X4), update_scales[c, g][:]
+            s = max(i for i in range(len(SCALE_RANGES)) if SCALE_RANGES[i][0] <= c)
+            offset = CHUNK * (c - SCALE_RANGES[s][0])
             if kind == "base":
-                return (
-                    base_codes[c, g].bitcast(FP4X4),
-                    base_planes[s][:, g, soff : soff + CHUNK],
-                )
-            if kind == "corr":
-                return (
-                    corr_codes[c, g].bitcast(FP8X4),
-                    corr_planes[s][CORR_PLANE_ROW:P, g, soff : soff + CHUNK],
-                )
-            return update_codes[c, g][:].bitcast(FP8X4), update_scales[c, g][:]
+                return base_codes[c, g].bitcast(FP4X4), base_planes[s][:, g, offset : offset + CHUNK]
+            return corr_codes[c, g].bitcast(FP8X4), corr_planes[s][CORR_PLANE_ROW:P, g, offset : offset + CHUNK]
 
-        sums, results = {}, {}
-
-        def multiply(c, j, kind, g, start, stop):
-            if start:
-                sums[c, j] = bank(4 * (c % 2) + j, [P, CHUNK])
-            codes, scales = moving(kind, c, g)
-            cols = slice(j * P, (j + 1) * P)
+        def multiply(into, c, j, term, a, b, start, stop):
+            codes, scales = moving_operand(term, c)
+            g = term[1]
+            rows = slice(j * P, (j + 1) * P)
             nc.tensor.matmul_mx(
-                out=sums[c, j][:],
-                lhsT=coef_codes[g][:, cols].bitcast(FP8X4),
-                lhsT_scale=coef_scales[g][:, cols],
-                rhs=codes,
-                rhs_scale=scales,
+                out=into[:],
+                lhsT=coef_codes[g][:, rows].bitcast(FP8X4),
+                lhsT_scale=coef_scales[g][:, rows],
+                rhs=codes[:, a:b],
+                rhs_scale=scales[:, a:b],
                 start=start,
                 stop=stop,
             )
 
+        sums = {}
+
+        def add_term(c, j, term, stop):
+            start = term == base_terms[0]
+            if start:
+                sums[c, j] = bank(ROW_TILES * (c % 2) + j, [P, CHUNK])
+            multiply(sums[c, j], c, j, term, 0, CHUNK, start, stop)
+
+        def sweep(c, terms, closing_term):
+            for term in terms:
+                for j in range(ROW_TILES):
+                    add_term(c, j, term, term == closing_term)
+
+        halves, results = [], {}
+        for h in range(2):
+            halves.append(kept("result%d" % h, [P, ROW_TILES, 2 * CHUNK], F32))
+            for c in (2 * h, 2 * h + 1):
+                results[c] = halves[h][:, :, CHUNK * (c % 2) : CHUNK * (c % 2 + 1)]
+
         def finish(c, j, a, b):
             piece = results[c][:, j, a:b]
-            nc.vector.tensor_tensor(
-                out=piece, in0=alpha_sb[c][:, j, a:b], in1=sums[c, j][:, a:b], op=ALU.subtract
+            nc.vector.tensor_tensor(out=piece, in0=alpha_sb[c][:, j, a:b], in1=sums[c, j][:, a:b], op=SUBTRACT)
+            nc.scalar.activation(out=piece, in_=piece, func=SQUARE)
+
+        def store(h, j0, j1, a, b):
+            nc.sync.dma_start(
+                out=out_rows[:, j0:j1, 2 * CHUNK * h + a : 2 * CHUNK * h + b], in_=halves[h][:, j0:j1, a:b]
             )
-            nc.scalar.activation(out=piece, in_=piece, func=ACT.Square)
 
-        def store(c, rows, a, b):
-            nc.sync.dma_start(out=out_rows[:, rows, c * CHUNK + a : c * CHUNK + b], in_=results[c][:, rows, a:b])
-
-        for c in range(CHUNKS):
-            results[c] = kept("result%d" % c, [P, ROW_TILES, CHUNK], F32)
-
-        terms = [(kind, g) for kind in ("base", "corr", "update") for g in range(PASSES)]
-
-        def sweep(c, some_terms, first, last):
-            for kind, g in some_terms:
-                for j in range(ROW_TILES):
-                    multiply(c, j, kind, g, (kind, g) == first, (kind, g) == last)
-
-        def finish_chunk(c):
+        closing = update_terms[-1]
+        prepare_coef(0, 1, 4)
+        sweep(0, [("base", 0)], closing)
+        prepare_coef(1, 2, 4)
+        sweep(0, [("corr", 0)], closing)
+        prepare_coef(2, 2, 6)
+        sweep(0, [("base", 1), ("corr", 1), ("base", 2), ("corr", 2)], closing)
+        sweep(1, base_terms + corr_terms, closing)
+        prepare_update((0, 1))
+        for term in update_terms:
+            for c in (0, 1):
+                sweep(c, [term], closing)
+        for c in (0, 1):
             for j in range(ROW_TILES):
                 finish(c, j, 0, CHUNK)
-            store(c, slice(0, ROW_TILES), 0, CHUNK)
+        store(0, 0, ROW_TILES, 0, 2 * CHUNK)
 
-        first, last = terms[0], terms[-1]
-        prepare_coef(0, 1, 4)
-        sweep(0, [("base", 0)], first, last)
-        prepare_coef(1, 2, 4)
-        sweep(0, [("corr", 0)], first, last)
-        prepare_coef(2, 2, 6)
-        for g in range(PASSES):
-            prepare_update(0, g)
-        sweep(0, [("base", 1), ("corr", 1), ("base", 2), ("corr", 2)] + terms[2 * PASSES :], first, last)
-
-        for c in (1, 2):
-            for g in range(PASSES):
-                prepare_update(c, g)
-            finish_chunk(c - 1)
-            sweep(c, terms, first, last)
-
-        c = CHUNKS - 1
-        for g in range(PASSES):
-            prepare_update(c, g)
-        finish_chunk(c - 1)
-        last_tile = ROW_TILES - 1
-        for term in terms[:PASSES]:
-            for j in range(ROW_TILES):
-                multiply(c, j, term[0], term[1], term == first, j == last_tile and term == terms[PASSES - 1])
-        tail = results[c][:, last_tile, :]
+        last_c, last_j = 3, ROW_TILES - 1
+        prepare_update((2, 3))
+        for c in (2, 3):
+            for term in base_terms:
+                for j in range(ROW_TILES):
+                    add_term(c, j, term, (c, j, term) == (last_c, last_j, base_terms[-1]))
+        for term in update_terms:
+            for c in (2, 3):
+                for j in range(ROW_TILES):
+                    if (c, j) != (last_c, last_j):
+                        add_term(c, j, term, False)
+        last_result = results[last_c][:, last_j, :]
         nc.vector.tensor_tensor(
-            out=tail, in0=alpha_sb[c][:, last_tile, :], in1=sums[c, last_tile][:], op=ALU.subtract
+            out=last_result, in0=alpha_sb[last_c][:, last_j, :], in1=sums[last_c, last_j][:], op=SUBTRACT
         )
-        for j in range(last_tile):
-            for term in terms[PASSES:]:
-                multiply(c, j, term[0], term[1], False, term == last)
-            finish(c, j, 0, CHUNK)
-            store(c, slice(j, j + 1), 0, CHUNK)
-        cols = slice(last_tile * P, M)
-        for index, (a, b) in enumerate(TAIL_PIECES):
+        for j in range(ROW_TILES):
+            for c in (2, 3):
+                if (c, j) != (last_c, last_j):
+                    for term in corr_terms:
+                        add_term(c, j, term, term == corr_terms[-1])
+                    for a, b in BANK_HALVES:
+                        finish(c, j, a, b)
+                    store(1, j, j + 1, CHUNK * (c % 2), CHUNK * (c % 2 + 1))
+        last_terms = update_terms + corr_terms
+        for index, (a, b) in enumerate(LAST_GROUPS):
             rest = bank(index, [P, b - a])
-            for kind, g in terms[PASSES:]:
-                codes, scales = moving(kind, c, g)
-                nc.tensor.matmul_mx(
-                    out=rest[:],
-                    lhsT=coef_codes[g][:, cols].bitcast(FP8X4),
-                    lhsT_scale=coef_scales[g][:, cols],
-                    rhs=codes[:, a:b],
-                    rhs_scale=scales[:, a:b],
-                    start=(kind, g) == terms[PASSES],
-                    stop=(kind, g) == last,
-                )
-            nc.vector.tensor_tensor(out=tail[:, a:b], in0=tail[:, a:b], in1=rest[:], op=ALU.subtract)
-            nc.scalar.activation(out=tail[:, a:b], in_=tail[:, a:b], func=ACT.Square)
-            store(c, slice(last_tile, ROW_TILES), a, b)
+            for term in last_terms:
+                multiply(rest, last_c, last_j, term, a, b, term == last_terms[0], term == last_terms[-1])
+            piece = last_result[:, a:b]
+            nc.vector.tensor_tensor(out=piece, in0=piece, in1=rest[:], op=SUBTRACT)
+            nc.scalar.activation(out=piece, in_=piece, func=SQUARE)
+            store(1, last_j, last_j + 1, CHUNK + a, CHUNK + b)

from contextlib import ExitStack

import concourse.mybir as mybir
from concourse.masks import make_identity

M, K, N = 512, 1536, 2048
FLOPS = 3 * 2 * M * K * N

F32 = mybir.dt.float32
BF16 = mybir.dt.bfloat16
I32 = mybir.dt.int32
U32 = mybir.dt.uint32
U8 = mybir.dt.uint8
FP8X4 = mybir.dt.float8_e4m3fn_x4
FP4X4 = mybir.dt.float4_e2m1fn_x4
SUBTRACT = mybir.AluOpType.subtract
SQUARE = mybir.ActivationFunctionType.Square

P = 128
PACK = 4
K_PASS = P * PACK
PASSES = K // K_PASS
ROW_TILES = M // P
CHUNK = 512
QUADRANT = 32
SCALE_ROWS = 4
ALIGN = 256

SCALE_RANGES = [(0, 1), (1, 2), (2, 4)]
CORR_PLANE_ROW = 4
VECTOR_COLS = 256
STAGE_BUFS = 3
BANK_HALVES = [(0, 256), (256, 512)]
LAST_GROUPS = [(0, 256), (256, 384), (384, 512)]


def tile_batch_pursuit_scores_s10_kernel(
    tc, alpha0, coef, base_words, base_scales, corr_words, corr_scales, update, out
):
    nc = tc.nc
    with ExitStack() as ctx:
        keep = ctx.enter_context(tc.tile_pool(name="keep", bufs=1))
        stage = ctx.enter_context(tc.tile_pool(name="stage", bufs=STAGE_BUFS))
        psum = ctx.enter_context(tc.psum_pool(name="psum", bufs=1))
        ctx.enter_context(tc.manual_schedule())

        def kept(name, shape, dtype):
            return keep.tile(shape, dtype, name=name, align_bytes=ALIGN)

        def bank(index, shape):
            return psum.tile(shape, F32, name="bank", tag="bank%d" % index)

        base_planes, corr_planes = [], []
        for s, (c0, c1) in enumerate(SCALE_RANGES):
            base_planes.append(kept("base_plane%d" % s, [P, PASSES, CHUNK * (c1 - c0)], U8))
            corr_planes.append(kept("corr_plane%d" % s, [P, PASSES, CHUNK * (c1 - c0)], U8))
        nc.gpsimd.memset(base_planes[0][:].bitcast(I32), 0)
        ident = kept("ident", [P, P], F32)
        make_identity(nc, ident[:])
        for plane in [corr_planes[0]] + base_planes[1:] + corr_planes[1:]:
            nc.vector.memset(plane[:].bitcast(I32), 0)

        coef_rows = coef.rearrange("(j p) k -> p j k", p=P)
        alpha_rows = alpha0.rearrange("(j p) n -> p j n", p=P)
        out_rows = out.rearrange("(j p) n -> p j n", p=P)
        base_rows = base_words.rearrange("g p b -> p g b")
        corr_rows = corr_words.rearrange("g p n t -> p g (n t)")

        coef_raw, base_codes, corr_codes, update_raw, alpha_sb = {}, {}, {}, {}, {}

        def load_scales(plane, first_row, scales, s):
            c0, c1 = SCALE_RANGES[s]
            for r in range(SCALE_ROWS):
                rows = scales[:, r : K_PASS // 32 : SCALE_ROWS, CHUNK * c0 : CHUNK * c1]
                nc.sync.dma_start(
                    out=plane[first_row + r : P : QUADRANT, :, :].bitcast(I32),
                    in_=rows.rearrange("g q n -> q g n").bitcast(I32),
                )

        def load_base_scales(s):
            load_scales(base_planes[s], 0, base_scales, s)

        def load_corr_scales(s):
            load_scales(corr_planes[s], CORR_PLANE_ROW, corr_scales, s)

        def load_coef(g, j0, j1):
            tile = kept("coef_raw%d_%d" % (g, j0), [P, j1 - j0, K_PASS], BF16)
            nc.sync.dma_start(out=tile[:], in_=coef_rows[:, j0:j1, g * K_PASS : (g + 1) * K_PASS])
            for j in range(j0, j1):
                coef_raw[g, j] = tile[:, j - j0, :]

        def load_base(c0, c1, g0, g1):
            tile = kept("base_codes%d_%d" % (c0, g0), [P, g1 - g0, 2 * CHUNK * (c1 - c0)], U8)
            nc.sync.dma_start(
                out=tile[:].bitcast(I32), in_=base_rows[:, g0:g1, 2 * CHUNK * c0 : 2 * CHUNK * c1].bitcast(I32)
            )
            for c in range(c0, c1):
                for g in range(g0, g1):
                    base_codes[c, g] = tile[:, g - g0, 2 * CHUNK * (c - c0) : 2 * CHUNK * (c - c0 + 1)]

        def load_corr(c0, c1, g0, g1):
            tile = kept("corr_codes%d_%d" % (c0, g0), [P, g1 - g0, CHUNK * (c1 - c0)], U32)
            nc.sync.dma_start(
                out=tile[:].bitcast(I32), in_=corr_rows[:, g0:g1, 4 * CHUNK * c0 : 4 * CHUNK * c1].bitcast(I32)
            )
            for c in range(c0, c1):
                for g in range(g0, g1):
                    corr_codes[c, g] = tile[:, g - g0, CHUNK * (c - c0) : CHUNK * (c - c0 + 1)]

        def load_update(c0, c1):
            for g in range(PASSES):
                tile = kept("update_raw%d_%d" % (c0, g), [P, PACK, CHUNK * (c1 - c0)], BF16)
                rows = update[g * K_PASS : (g + 1) * K_PASS, CHUNK * c0 : CHUNK * c1]
                nc.sync.dma_start(out=tile[:], in_=rows.rearrange("(p t) n -> p t n", t=PACK))
                for c in range(c0, c1):
                    update_raw[c, g] = tile[:, :, CHUNK * (c - c0) : CHUNK * (c - c0 + 1)]

        def load_alpha(c0, c1):
            tile = kept("alpha%d" % c0, [P, ROW_TILES, CHUNK * (c1 - c0)], BF16)
            nc.sync.dma_start(out=tile[:], in_=alpha_rows[:, :, CHUNK * c0 : CHUNK * c1])
            for c in range(c0, c1):
                alpha_sb[c] = tile[:, :, CHUNK * (c - c0) : CHUNK * (c - c0 + 1)]

        load_coef(0, 0, 2)
        load_coef(0, 2, ROW_TILES)
        load_base_scales(0)
        load_base(0, 1, 0, 1)
        load_coef(1, 0, ROW_TILES)
        load_corr_scales(0)
        load_corr(0, 1, 0, 1)
        load_coef(2, 0, ROW_TILES)
        load_base(0, 1, 1, PASSES)
        load_corr(0, 1, 1, PASSES)
        load_base_scales(1)
        load_base(1, 2, 0, PASSES)
        load_corr_scales(1)
        load_corr(1, 2, 0, PASSES)
        load_update(0, 2)
        load_alpha(0, 2)
        load_base_scales(2)
        load_base(2, 4, 0, PASSES)
        load_update(2, 4)
        load_corr_scales(2)
        load_corr(2, 4, 0, PASSES)
        load_alpha(2, 4)

        coef_codes, coef_scales, update_codes, update_scales = {}, {}, {}, {}

        def prepare_coef(g, tiles_per_bank, first_bank):
            coef_codes[g] = kept("coef_codes%d" % g, [P, M], U32)
            coef_scales[g] = kept("coef_scales%d" % g, [P, M], U8)
            for part in range(ROW_TILES // tiles_per_bank):
                turned = bank(first_bank + part, [P, tiles_per_bank, 2, P])
                for jj in range(tiles_per_bank):
                    pairs = coef_raw[g, tiles_per_bank * part + jj].bitcast(F32)
                    for u in range(2):
                        nc.tensor.transpose(turned[:, jj, u, :], pairs[:, u : 2 * P : 2], ident[:])
                grouped = stage.tile([P, tiles_per_bank * K_PASS], BF16, name="coef_grouped", align_bytes=ALIGN)
                nc.scalar.copy(
                    out=grouped[:].bitcast(F32).rearrange("p (j m u) -> p j m u", j=tiles_per_bank, u=2),
                    in_=turned[:].rearrange("p j u m -> p j m u"),
                )
                rows = slice(part * tiles_per_bank * P, (part + 1) * tiles_per_bank * P)
                nc.vector.quantize_mx(
                    out=coef_codes[g][:, rows].bitcast(FP8X4), scales=coef_scales[g][:, rows], in_=grouped[:]
                )

        def interleave_update(c, g):
            grouped = stage.tile([P, CHUNK, PACK], BF16, name="update_grouped", align_bytes=ALIGN)
            for copy, a, b in ((nc.vector.tensor_copy, 0, VECTOR_COLS), (nc.scalar.copy, VECTOR_COLS, CHUNK)):
                copy(
                    out=grouped[:, a:b, :].rearrange("p (n i) t -> p n t i", i=4),
                    in_=update_raw[c, g][:, :, a:b].rearrange("p t (n i) -> p n t i", i=4),
                )
            return grouped

        def quantize_update(c, g, grouped):
            update_codes[c, g] = kept("update_codes%d_%d" % (c, g), [P, CHUNK], U32)
            update_scales[c, g] = kept("update_scales%d_%d" % (c, g), [P, CHUNK], U8)
            nc.vector.quantize_mx(
                out=update_codes[c, g][:].bitcast(FP8X4),
                scales=update_scales[c, g][:],
                in_=grouped[:].rearrange("p n t -> p (n t)"),
            )

        def prepare_update(chunks):
            waiting = None
            for g in range(PASSES):
                for c in chunks:
                    grouped = interleave_update(c, g)
                    if waiting is not None:
                        quantize_update(*waiting)
                    waiting = (c, g, grouped)
            quantize_update(*waiting)

        base_terms = [("base", g) for g in range(PASSES)]
        corr_terms = [("corr", g) for g in range(PASSES)]
        update_terms = [("update", g) for g in range(PASSES)]

        def moving_operand(term, c):
            kind, g = term
            if kind == "update":
                return update_codes[c, g][:].bitcast(FP8X4), update_scales[c, g][:]
            s = max(i for i in range(len(SCALE_RANGES)) if SCALE_RANGES[i][0] <= c)
            offset = CHUNK * (c - SCALE_RANGES[s][0])
            if kind == "base":
                return base_codes[c, g].bitcast(FP4X4), base_planes[s][:, g, offset : offset + CHUNK]
            return corr_codes[c, g].bitcast(FP8X4), corr_planes[s][CORR_PLANE_ROW:P, g, offset : offset + CHUNK]

        def multiply(into, c, j, term, a, b, start, stop):
            codes, scales = moving_operand(term, c)
            g = term[1]
            rows = slice(j * P, (j + 1) * P)
            nc.tensor.matmul_mx(
                out=into[:],
                lhsT=coef_codes[g][:, rows].bitcast(FP8X4),
                lhsT_scale=coef_scales[g][:, rows],
                rhs=codes[:, a:b],
                rhs_scale=scales[:, a:b],
                start=start,
                stop=stop,
            )

        sums = {}

        def add_term(c, j, term, stop):
            start = term == base_terms[0]
            if start:
                sums[c, j] = bank(ROW_TILES * (c % 2) + j, [P, CHUNK])
            multiply(sums[c, j], c, j, term, 0, CHUNK, start, stop)

        def sweep(c, terms, closing_term):
            for term in terms:
                for j in range(ROW_TILES):
                    add_term(c, j, term, term == closing_term)

        halves, results = [], {}
        for h in range(2):
            halves.append(kept("result%d" % h, [P, ROW_TILES, 2 * CHUNK], F32))
            for c in (2 * h, 2 * h + 1):
                results[c] = halves[h][:, :, CHUNK * (c % 2) : CHUNK * (c % 2 + 1)]

        def finish(c, j, a, b):
            piece = results[c][:, j, a:b]
            nc.vector.tensor_tensor(out=piece, in0=alpha_sb[c][:, j, a:b], in1=sums[c, j][:, a:b], op=SUBTRACT)
            nc.scalar.activation(out=piece, in_=piece, func=SQUARE)

        def store(h, j0, j1, a, b):
            nc.sync.dma_start(
                out=out_rows[:, j0:j1, 2 * CHUNK * h + a : 2 * CHUNK * h + b], in_=halves[h][:, j0:j1, a:b]
            )

        closing = update_terms[-1]
        prepare_coef(0, 1, 4)
        sweep(0, [("base", 0)], closing)
        prepare_coef(1, 2, 4)
        sweep(0, [("corr", 0)], closing)
        prepare_coef(2, 2, 6)
        sweep(0, [("base", 1), ("corr", 1), ("base", 2), ("corr", 2)], closing)
        sweep(1, base_terms + corr_terms, closing)
        prepare_update((0, 1))
        for term in update_terms:
            for c in (0, 1):
                sweep(c, [term], closing)
        for c in (0, 1):
            for j in range(ROW_TILES):
                finish(c, j, 0, CHUNK)
        store(0, 0, ROW_TILES, 0, 2 * CHUNK)

        last_c, last_j = 3, ROW_TILES - 1
        prepare_update((2, 3))
        for c in (2, 3):
            for term in base_terms:
                for j in range(ROW_TILES):
                    add_term(c, j, term, (c, j, term) == (last_c, last_j, base_terms[-1]))
        for term in update_terms:
            for c in (2, 3):
                for j in range(ROW_TILES):
                    if (c, j) != (last_c, last_j):
                        add_term(c, j, term, False)
        last_result = results[last_c][:, last_j, :]
        nc.vector.tensor_tensor(
            out=last_result, in0=alpha_sb[last_c][:, last_j, :], in1=sums[last_c, last_j][:], op=SUBTRACT
        )
        for j in range(ROW_TILES):
            for c in (2, 3):
                if (c, j) != (last_c, last_j):
                    for term in corr_terms:
                        add_term(c, j, term, term == corr_terms[-1])
                    for a, b in BANK_HALVES:
                        finish(c, j, a, b)
                    store(1, j, j + 1, CHUNK * (c % 2), CHUNK * (c % 2 + 1))
        last_terms = update_terms + corr_terms
        for index, (a, b) in enumerate(LAST_GROUPS):
            rest = bank(index, [P, b - a])
            for term in last_terms:
                multiply(rest, last_c, last_j, term, a, b, term == last_terms[0], term == last_terms[-1])
            piece = last_result[:, a:b]
            nc.vector.tensor_tensor(out=piece, in0=piece, in1=rest[:], op=SUBTRACT)
            nc.scalar.activation(out=piece, in_=piece, func=SQUARE)
            store(1, last_j, last_j + 1, CHUNK + a, CHUNK + b)
